import numpy as np
import ml_dtypes


def mxq(x, axis, fmt="e4m3"):
    dtype, down = {"e4m3": (ml_dtypes.float8_e4m3fn, 7), "e5m2": (ml_dtypes.float8_e5m2, 14)}[fmt]
    v = np.moveaxis(np.asarray(x, np.float32).astype(ml_dtypes.bfloat16).astype(np.float64), axis, -1)
    blocks = v.reshape(v.shape[:-1] + (-1, 32))
    amax = np.abs(blocks).max(-1, keepdims=True)
    byte = np.maximum(np.where(amax > 0, np.frexp(amax)[1] - 1 + 127, 0) - down, 1)
    scale = np.exp2(byte - 127.0)
    codes = (blocks / scale).astype(np.float32).astype(dtype).astype(np.float64)
    return np.moveaxis((codes * scale).reshape(v.shape), -1, axis)


WIDE = False


def mx_kscale(k):
    if not WIDE:
        return np.ones(k)
    levels = np.array([24, -24, 12, -12, 0])
    if k % 512:
        return np.exp2(np.random.permutation(np.resize(levels, k // 32))).repeat(32)
    a = np.empty((k // 512, 16))
    for p in range(k // 512):
        a[p, :8] = np.random.permutation(np.resize(levels, 8))
        for g in range(8):
            far = levels[np.abs(levels - a[p, g]) >= 10]
            a[p, g + 8] = far[np.random.randint(len(far))]
    return np.exp2(a.ravel()).repeat(32)


def f64(x):
    return np.asarray(x).astype(np.float64)


def striped(idx):
    return np.tile(idx.reshape(-1, 16).T, (8, 1)).astype(np.uint16)


def unstriped(offs):
    return offs[:16].T.reshape(-1).astype(np.int64)


def striped8(idx):
    return np.concatenate([v.reshape(-1, 16).T for v in idx]).astype(np.uint16)


def unstriped8(offs):
    return np.stack([offs[16 * g:16 * g + 16].T.reshape(-1) for g in range(8)]).astype(np.int64)


E2M1 = np.array([0.0, 0.5, 1.0, 1.5, 2.0, 3.0, 4.0, 6.0, -0.0, -0.5, -1.0, -1.5, -2.0, -3.0, -4.0, -6.0])


def pack_weight(w, fmt):
    k, n = w.shape
    w = f64(np.asarray(w, np.float32).astype(ml_dtypes.bfloat16)).reshape(k // 32, 32, n)
    amax = np.abs(w).max(1)
    if fmt == "e4m3":
        byte = np.frexp(amax)[1] - 1 + 127 - 7
    else:
        mant, ex = np.frexp(amax / 6.0)
        byte = np.where(mant > 0.5, ex, ex - 1) + 127
    byte = np.clip(np.where(amax > 0, byte, 1), 1, 254)
    scaled = (w * np.exp2(127.0 - byte)[:, None, :]).reshape(k, n).astype(np.float32)
    by_word = np.ascontiguousarray(scaled.reshape(k // 512, 128, 4, n).transpose(0, 1, 3, 2))
    if fmt == "e4m3":
        words = by_word.astype(ml_dtypes.float8_e4m3fn).view(np.uint8)
    else:
        c = by_word.astype(ml_dtypes.float4_e2m1fn).view(np.uint8) & 0xF
        words = (c[..., 0::2] | (c[..., 1::2] << 4)).reshape(k // 512, 128, 2 * n)
    return np.ascontiguousarray(words), np.ascontiguousarray(byte.astype(np.uint8).reshape(k // 512, 16, n))


def unpack_weight(words, scales, fmt):
    g, _, n = scales.shape
    words = np.ascontiguousarray(words).reshape(g, 128, n, -1)
    if fmt == "e4m3":
        vals = words.view(ml_dtypes.float8_e4m3fn).astype(np.float64)
    else:
        nib = np.empty((g, 128, n, 4), np.uint8)
        nib[..., 0::2] = words & 0xF
        nib[..., 1::2] = words >> 4
        vals = E2M1[nib]
    vals = vals * np.repeat(np.exp2(scales.astype(np.float64) - 127.0), 8, axis=1)[..., None]
    return vals.transpose(0, 1, 3, 2).reshape(g * 512, n)


def pack_table4(v):
    words, scales = pack_weight(v, "e2m1")
    g, t = words.shape[0] // 2, v.shape[1]
    return np.ascontiguousarray(words.reshape(g, 2, 128, t, 2).transpose(0, 2, 3, 1, 4).reshape(g, 128, t, 4)), scales


def unpack_table4(words, scales):
    g, _, t, _ = words.shape
    return unpack_weight(words.reshape(g, 128, t, 2, 2).transpose(0, 3, 1, 2, 4).reshape(2 * g, 128, 2 * t), scales, "e2m1")


def planes(y):
    n, m = y.shape
    v = y.astype(np.float32).astype(ml_dtypes.bfloat16).astype(np.float64).reshape(n // 32, 32, m)
    top = np.abs(v).max(1)
    byte = np.clip(np.where(top > 0, np.frexp(top)[1] - 1 + 127 - 7, 1), 1, 254)
    codes = (v * np.exp2(127.0 - byte)[:, None, :]).reshape(n, m).astype(np.float32).astype(ml_dtypes.float8_e4m3fn).view(np.uint8)
    words = codes.reshape(n // 512, 128, 4, m).transpose(0, 1, 3, 2)
    return np.ascontiguousarray(words), np.ascontiguousarray(byte.astype(np.uint8).reshape(n // 512, 16, m))


def sigm(f):
    return 1.0 / (1.0 + np.exp(-np.maximum(f, -700.0)))


K, L, R, N, T, J = 512, 1024, 512, 512, 2048, 1024


def setup_inputs():
    n = np.random.standard_normal
    s = mx_kscale(K)[:, None]
    s2 = mx_kscale(L)[:, None]
    u = mx_kscale(R)[:, None]
    p_tab = pack_table4(n((L, T)) * s2)
    p_wa = pack_weight(n((K, R)) / np.sqrt(K) / s * u.T, "e4m3")
    p_wb = pack_weight(n((L, R)) / np.sqrt(L) / s2, "e4m3")
    p_wd = pack_weight(n((R, N)) / np.sqrt(R) / u, "e4m3")
    return {
        "tab_words": p_tab[0],
        "tab_scales": p_tab[1],
        "xT": (n((K, T)) * s).astype(np.float32),
        "wgt2": np.repeat(np.random.uniform(0.5, 2.0, (8, J)), 16, axis=0).astype(np.float32),
        "wa_words": p_wa[0],
        "wa_scales": p_wa[1],
        "wb_words": p_wb[0],
        "wb_scales": p_wb[1],
        "wd_words": p_wd[0],
        "wd_scales": p_wd[1],
        "b": (0.3 * n(N)).astype(np.float32),
        "offs": striped(np.random.permutation(T)[:J]),
        "offs2": striped8(np.stack([np.random.permutation(T)[:J] for _ in range(8)])),
    }


def reference(tab_words, tab_scales, xT, wgt2, wa_words, wa_scales, wb_words, wb_scales, wd_words, wd_scales, b, offs, offs2):
    idx = unstriped(offs)
    idx2 = unstriped8(offs2)
    tab_ = unpack_table4(tab_words, tab_scales)[:, idx]
    rows = np.arange(K)
    xg = f64(wgt2)[rows // 4 % 128] * f64(xT)[rows[:, None], idx2[rows % 512 // 64]]
    xT_ = mxq(xg, 0, "e4m3")
    wa_ = unpack_weight(wa_words, wa_scales, "e4m3")
    wb_ = unpack_weight(wb_words, wb_scales, "e4m3")
    ya = wa_.T @ xT_
    yb = wb_.T @ tab_
    h = ya * sigm(yb)
    h_ = mxq(h, 0, "e4m3")
    wd_ = unpack_weight(wd_words, wd_scales, "e4m3")
    y = wd_.T @ h_
    out_0 = y + f64(b)[:, None]
    return (out_0,) + planes(out_0)

@@ -1,0 +1,246 @@
+from contextlib import ExitStack
+
+import concourse.mybir as mybir
+
+K, L, R, N, T, J = 512, 1024, 512, 512, 2048, 1024
+FLOPS = 2 * J * (K * R + L * R + R * N)
+
+F32 = mybir.dt.float32
+BF16 = mybir.dt.bfloat16
+I32 = mybir.dt.int32
+U32 = mybir.dt.uint32
+U16 = mybir.dt.uint16
+U8 = mybir.dt.uint8
+FP8X4 = mybir.dt.float8_e4m3fn_x4
+FP4X4 = mybir.dt.float4_e2m1fn_x4
+ACT = mybir.ActivationFunctionType
+MULT = mybir.AluOpType.mult
+
+P = 128
+PACK = 4
+QUADS = 4
+BANK = 512
+SUB = BANK // PACK
+CHUNKS = [256, 256, 256, 256]
+HALF = J // 2
+
+
+def tile_list_htabg_gate_biasP_kernel(
+    tc, tab_words, tab_scales, xT, wgt2, wa_words, wa_scales, wb_words, wb_scales, wd_words, wd_scales, b, offs, offs2,
+    out_0, out_1, out_2,
+):
+    nc = tc.nc
+    with ExitStack() as ctx:
+        keep = ctx.enter_context(tc.tile_pool(name="keep", bufs=1))
+        ring = ctx.enter_context(tc.tile_pool(name="ring", bufs=3))
+        stage_pool = ctx.enter_context(tc.tile_pool(name="stage", bufs=1))
+        psum = ctx.enter_context(tc.psum_pool(name="psum", bufs=4))
+
+        def held(shape, dtype, name):
+            return keep.tile(shape, dtype, name=name, align_bytes=64)
+
+        def words_of(dram, a):
+            return dram[a].rearrange("p n i -> p (n i)").bitcast(I32)
+
+        def staged(shape, dtype, name, kib):
+            return stage_pool.tile(shape, dtype, name=name, align_bytes=64, offset=kib * 1024)
+
+        def deal_words(raw, name):
+            dealt = held([P, R], U32, name)
+            nc.scalar.copy(
+                dealt[:].rearrange("p (t m i) -> p m t i", t=PACK, i=4),
+                raw.bitcast(U32).rearrange("p (m i t) -> p m t i", t=PACK, i=4),
+            )
+            return dealt
+
+        idx = keep.tile([P, J // 16], U16, name="idx")
+        idx2 = keep.tile([P, J // 16], U16, name="idx2")
+        w_s_raw = staged([P, R], U8, "w_s_raw", 0)
+        tab_s = staged([P, T], U8, "tab_s", 8)
+        wb_raw = staged([P, 2, R], I32, "wb_raw", 16)
+        tab_w = staged([P, T], I32, "tab_w", 24)
+        w_s = held([P, 4 * R], U8, "w_s")
+        v_s = held([P, 2 * J], U8, "v_s")
+        nc.vector.memset(w_s_raw[64:, :].bitcast(I32), 0)
+        nc.vector.memset(tab_s[32:64, :].bitcast(I32), 0)
+        nc.vector.memset(tab_s[64:, :].bitcast(I32), 0)
+        nc.vector.memset(w_s[:].bitcast(I32), 0)
+        nc.vector.memset(v_s[:].bitcast(I32), 0)
+
+        nc.sync.dma_start(idx[:], offs)
+        nc.sync.dma_start(tab_s[:32, :].bitcast(I32), tab_scales.bitcast(I32).rearrange("a q n -> q a n"))
+        for k, rows in enumerate((wb_scales[0], wb_scales[1], wa_scales[0], wd_scales[0])):
+            nc.sync.dma_start(w_s_raw[k:64:4, :].bitcast(I32), rows.bitcast(I32))
+        nc.sync.dma_start(tab_w[:], words_of(tab_words, 0))
+        nc.sync.dma_start(wb_raw[:], wb_words.rearrange("a p n i -> p a (n i)").bitcast(I32))
+        wgt_lo = held([P, HALF], F32, "wgt_lo")
+        nc.sync.dma_start(wgt_lo[:], wgt2[:, :HALF])
+        nc.sync.dma_start(idx2[:], offs2)
+        bias = held([P, PACK], F32, "bias")
+        nc.gpsimd.dma_start(bias[:], b.rearrange("(p t) -> p t", t=PACK))
+
+        w_s_dealt = held([P, R], U8, "w_s_dealt")
+        nc.vector.tensor_copy(
+            w_s_dealt[:].rearrange("p (t m) -> p t m", t=PACK), w_s_raw[:].rearrange("p (m t) -> p t m", t=PACK)
+        )
+        for q in range(QUADS):
+            nc.scalar.dma_start(w_s[32 * q : 32 * q + 4, :].bitcast(I32), w_s_dealt[16 * q : 16 * q + 16, :].bitcast(I32))
+
+        x_rows = xT.rearrange("(p i) t -> p i t", i=PACK)
+        x_planes = []
+
+        def load_x(i):
+            plane = staged([P, T], F32, "x%d" % i, 8 * i)
+            nc.sync.dma_start(plane[:], x_rows[:, i, :])
+            x_planes.append(plane)
+
+        load_x(0)
+        v_s_picked = held([P, J], U8, "v_s_picked")
+        nc.vector.tensor_copy(v_s_picked[:], tab_s[:].indirect(idx[:]))
+        for q in range(QUADS):
+            nc.scalar.dma_start(v_s[32 * q : 32 * q + 4, :].bitcast(I32), v_s_picked[8 * q : 8 * q + 8, :].bitcast(I32))
+        load_x(1)
+        wb = [deal_words(wb_raw[:, a, :], "wb%d" % a) for a in range(2)]
+        load_x(2)
+        both = staged([P, J], U32, "v_both", 33)
+        nc.vector.tensor_copy(both[:], tab_w[:].bitcast(U32).indirect(idx[:]))
+        load_x(3)
+        v_w = []
+        for u in range(2):
+            parted = held([P, 2, HALF], U16, "v_w%d" % u)
+            nc.vector.tensor_copy(
+                parted[:], both[:, u * HALF : (u + 1) * HALF].bitcast(U16).rearrange("p (j d) -> p d j", d=2)
+            )
+            v_w.append(parted)
+        wa_raw = staged([P, R], I32, "wa_raw", 32)
+        wgt_hi = staged([P, HALF], F32, "wgt_hi", 34)
+        wd_raw = staged([P, N], I32, "wd_raw", 36)
+        nc.sync.dma_start(wa_raw[:], words_of(wa_words, 0))
+        nc.sync.dma_start(wgt_hi[:], wgt2[:, HALF:])
+        nc.sync.dma_start(wd_raw[:], words_of(wd_words, 0))
+        wgt = [wgt_lo, wgt_hi]
+
+        gates = []
+        for s in range(J // SUB):
+            u, j0 = divmod(s * SUB, HALF)
+            yb = psum.tile([P, PACK, SUB], F32, name="yb", tag="first")
+            for t in range(PACK):
+                for a in range(2):
+                    nc.tensor.matmul_mx(
+                        out=yb[:, t, :],
+                        lhsT=wb[a][:, t * P : (t + 1) * P].bitcast(FP8X4),
+                        lhsT_scale=w_s[:, a * R + t * P : a * R + (t + 1) * P],
+                        rhs=v_w[u][:, a, j0 : j0 + SUB].bitcast(FP4X4),
+                        rhs_scale=v_s[:, a * J + s * SUB : a * J + (s + 1) * SUB],
+                        start=(a == 0),
+                        stop=(a == 1),
+                    )
+            gate = held([P, SUB, PACK], F32, "gate%d" % s)
+            nc.scalar.activation(gate[:], yb[:].rearrange("p t j -> p j t"), ACT.Sigmoid)
+            gates.append(gate)
+
+        y_words = held([P, J], I32, "y_words")
+        y_scales = held([P, J], U8, "y_scales")
+        out_rows = out_0.rearrange("(p t) j -> p t j", t=PACK)
+        out_words = words_of(out_1, 0)
+
+        def interleave(copy, dst, src):
+            copy(
+                dst.rearrange("p (c i t) -> p c t i", t=PACK, i=4),
+                src.rearrange("p t (c i) -> p c t i", i=4),
+            )
+
+        starts = [sum(CHUNKS[:c]) for c in range(len(CHUNKS))]
+        xq = {}
+        hq = {}
+        yb16 = {}
+
+        def pick(c):
+            j0, w = starts[c], CHUNKS[c]
+            u, h0 = divmod(j0, HALF)
+            picked = ring.tile([P, PACK, w], F32, name="picked", align_bytes=64)
+            for i in range(PACK):
+                nc.vector.tensor_tensor(
+                    picked[:, i, :], x_planes[i][:].indirect(idx2[:, j0 // 16 : (j0 + w) // 16]), wgt[u][:, h0 : h0 + w], MULT
+                )
+            x16 = held([P, PACK * w], BF16, "x16_%d" % c)
+            interleave(nc.scalar.copy, x16[:], picked[:])
+            xq[c] = x16
+
+        def quantise(src, name, w):
+            codes = held([P, w], U32, name + "_codes")
+            scales = held([P, w], U8, name + "_scales")
+            nc.vector.quantize_mx(out=codes[:].bitcast(FP8X4), scales=scales[:], in_=src[:])
+            return codes, scales
+
+        def first_layer(c):
+            j0, w = starts[c], CHUNKS[c]
+            codes, scales = quantise(xq[c], "x%d" % c, w)
+            h16 = held([P, PACK * w], BF16, "h16_%d" % c)
+            for s in range(w // SUB):
+                cols = slice(s * SUB, (s + 1) * SUB)
+                ya = psum.tile([P, PACK, SUB], F32, name="ya", tag="first")
+                for t in range(PACK):
+                    nc.tensor.matmul_mx(
+                        out=ya[:, t, :],
+                        lhsT=wa[:, t * P : (t + 1) * P].bitcast(FP8X4),
+                        lhsT_scale=w_s[:, 2 * R + t * P : 2 * R + (t + 1) * P],
+                        rhs=codes[:, cols].bitcast(FP8X4),
+                        rhs_scale=scales[:, cols],
+                        start=True,
+                        stop=True,
+                    )
+                nc.vector.tensor_tensor(
+                    h16[:, s * BANK : (s + 1) * BANK].rearrange("p (j t) -> p j t", t=PACK),
+                    ya[:].rearrange("p t j -> p j t"),
+                    gates[j0 // SUB + s][:],
+                    MULT,
+                )
+            hq[c] = h16
+
+        def second_layer(c):
+            j0, w = starts[c], CHUNKS[c]
+            codes, scales = quantise(hq[c], "h%d" % c, w)
+            y32 = held([P, PACK, w], F32, "y32_%d" % c)
+            per_bank = BANK // w
+            for t0 in range(0, PACK, per_bank):
+                y = psum.tile([P, per_bank, w], F32, name="y", tag="second")
+                for t in range(t0, t0 + per_bank):
+                    nc.tensor.matmul_mx(
+                        out=y[:, t - t0, :],
+                        lhsT=wd[:, t * P : (t + 1) * P].bitcast(FP8X4),
+                        lhsT_scale=w_s[:, 3 * R + t * P : 3 * R + (t + 1) * P],
+                        rhs=codes[:].bitcast(FP8X4),
+                        rhs_scale=scales[:],
+                        start=True,
+                        stop=True,
+                    )
+                for t in range(t0, t0 + per_bank):
+                    nc.scalar.activation(y32[:, t, :], y[:, t - t0, :], ACT.Identity, bias=bias[:, t : t + 1])
+            nc.sync.dma_start(out_rows[:, :, j0 : j0 + w], y32[:])
+            y16 = held([P, PACK * w], BF16, "y16_%d" % c)
+            interleave(nc.scalar.copy if c == 0 else nc.vector.tensor_copy, y16[:], y32[:])
+            yb16[c] = y16
+
+        def planes(c):
+            j0, w = starts[c], CHUNKS[c]
+            nc.vector.quantize_mx(
+                out=y_words[:, j0 : j0 + w].bitcast(FP8X4), scales=y_scales[:, j0 : j0 + w], in_=yb16[c][:]
+            )
+            nc.sync.dma_start(out_words[:, j0 : j0 + w], y_words[:, j0 : j0 + w])
+
+        n = len(CHUNKS)
+        pick(0)
+        wa = deal_words(wa_raw[:], "wa")
+        pick(1)
+        wd = deal_words(wd_raw[:], "wd")
+        for c in range(2, n):
+            pick(c)
+        stages = [planes, second_layer, first_layer]
+        for step in range(n + len(stages) - 1):
+            for depth, stage in enumerate(stages):
+                c = step - (len(stages) - 1 - depth)
+                if 0 <= c < n:
+                    stage(c)
+        for q in range(QUADS):
+            nc.sync.dma_start(out_2[0, 4 * q : 4 * q + 4, :].bitcast(I32), y_scales[32 * q : 32 * q + 4, :].bitcast(I32))

@@ -23,6 +23,7 @@ BANK = 512
 SUB = BANK // PACK
 CHUNKS = [256, 256, 256, 256]
 HALF = J // 2
+EARLY = 768
 
 
 def tile_list_htabg_gate_biasP_kernel(
@@ -32,7 +33,6 @@ def tile_list_htabg_gate_biasP_kernel(
     nc = tc.nc
     with ExitStack() as ctx:
         keep = ctx.enter_context(tc.tile_pool(name="keep", bufs=1))
-        ring = ctx.enter_context(tc.tile_pool(name="ring", bufs=3))
         stage_pool = ctx.enter_context(tc.tile_pool(name="stage", bufs=1))
         psum = ctx.enter_context(tc.psum_pool(name="psum", bufs=4))
 
@@ -67,14 +67,14 @@ def tile_list_htabg_gate_biasP_kernel(
         nc.vector.memset(w_s[:].bitcast(I32), 0)
         nc.vector.memset(v_s[:].bitcast(I32), 0)
 
-        nc.sync.dma_start(idx[:], offs)
-        nc.sync.dma_start(tab_s[:32, :].bitcast(I32), tab_scales.bitcast(I32).rearrange("a q n -> q a n"))
         for k, rows in enumerate((wb_scales[0], wb_scales[1], wa_scales[0], wd_scales[0])):
             nc.sync.dma_start(w_s_raw[k:64:4, :].bitcast(I32), rows.bitcast(I32))
+        nc.sync.dma_start(idx[:], offs)
+        nc.sync.dma_start(tab_s[:32, :].bitcast(I32), tab_scales.bitcast(I32).rearrange("a q n -> q a n"))
         nc.sync.dma_start(tab_w[:], words_of(tab_words, 0))
         nc.sync.dma_start(wb_raw[:], wb_words.rearrange("a p n i -> p a (n i)").bitcast(I32))
-        wgt_lo = held([P, HALF], F32, "wgt_lo")
-        nc.sync.dma_start(wgt_lo[:], wgt2[:, :HALF])
+        wgt_lo = held([P, EARLY], F32, "wgt_lo")
+        nc.sync.dma_start(wgt_lo[:], wgt2[:, :EARLY])
         nc.sync.dma_start(idx2[:], offs2)
         bias = held([P, PACK], F32, "bias")
         nc.gpsimd.dma_start(bias[:], b.rearrange("(p t) -> p t", t=PACK))
@@ -84,7 +84,7 @@ def tile_list_htabg_gate_biasP_kernel(
             w_s_dealt[:].rearrange("p (t m) -> p t m", t=PACK), w_s_raw[:].rearrange("p (m t) -> p t m", t=PACK)
         )
         for q in range(QUADS):
-            nc.scalar.dma_start(w_s[32 * q : 32 * q + 4, :].bitcast(I32), w_s_dealt[16 * q : 16 * q + 16, :].bitcast(I32))
+            nc.sync.dma_start(w_s[32 * q : 32 * q + 4, :].bitcast(I32), w_s_dealt[16 * q : 16 * q + 16, :].bitcast(I32))
 
         x_rows = xT.rearrange("(p i) t -> p i t", i=PACK)
         x_planes = []
@@ -98,7 +98,7 @@ def tile_list_htabg_gate_biasP_kernel(
         v_s_picked = held([P, J], U8, "v_s_picked")
         nc.vector.tensor_copy(v_s_picked[:], tab_s[:].indirect(idx[:]))
         for q in range(QUADS):
-            nc.scalar.dma_start(v_s[32 * q : 32 * q + 4, :].bitcast(I32), v_s_picked[8 * q : 8 * q + 8, :].bitcast(I32))
+            nc.sync.dma_start(v_s[32 * q : 32 * q + 4, :].bitcast(I32), v_s_picked[8 * q : 8 * q + 8, :].bitcast(I32))
         load_x(1)
         wb = [deal_words(wb_raw[:, a, :], "wb%d" % a) for a in range(2)]
         load_x(2)
@@ -113,10 +113,10 @@ def tile_list_htabg_gate_biasP_kernel(
             )
             v_w.append(parted)
         wa_raw = staged([P, R], I32, "wa_raw", 32)
-        wgt_hi = staged([P, HALF], F32, "wgt_hi", 34)
+        wgt_hi = staged([P, J - EARLY], F32, "wgt_hi", 34)
         wd_raw = staged([P, N], I32, "wd_raw", 36)
         nc.sync.dma_start(wa_raw[:], words_of(wa_words, 0))
-        nc.sync.dma_start(wgt_hi[:], wgt2[:, HALF:])
+        nc.sync.dma_start(wgt_hi[:], wgt2[:, EARLY:])
         nc.sync.dma_start(wd_raw[:], words_of(wd_words, 0))
         wgt = [wgt_lo, wgt_hi]
 
@@ -157,14 +157,22 @@ def tile_list_htabg_gate_biasP_kernel(
 
         def pick(c):
             j0, w = starts[c], CHUNKS[c]
-            u, h0 = divmod(j0, HALF)
-            picked = ring.tile([P, PACK, w], F32, name="picked", align_bytes=64)
-            for i in range(PACK):
-                nc.vector.tensor_tensor(
-                    picked[:, i, :], x_planes[i][:].indirect(idx2[:, j0 // 16 : (j0 + w) // 16]), wgt[u][:, h0 : h0 + w], MULT
-                )
+            u, h0 = divmod(j0, EARLY)
             x16 = held([P, PACK * w], BF16, "x16_%d" % c)
-            interleave(nc.scalar.copy, x16[:], picked[:])
+            group = 2 if u == 0 else PACK
+            for i0 in range(0, PACK, group):
+                picked = held([P, group, w], F32, "picked%d_%d" % (c, i0))
+                for i in range(i0, i0 + group):
+                    nc.vector.tensor_tensor(
+                        picked[:, i - i0, :],
+                        x_planes[i][:].indirect(idx2[:, j0 // 16 : (j0 + w) // 16]),
+                        wgt[u][:, h0 : h0 + w],
+                        MULT,
+                    )
+                nc.scalar.copy(
+                    x16[:].rearrange("p (c i t) -> p c t i", t=PACK, i=4)[:, :, i0 : i0 + group, :],
+                    picked[:].rearrange("p t (c i) -> p c t i", i=4),
+                )
             xq[c] = x16
 
         def quantise(src, name, w):
@@ -218,14 +226,14 @@ def tile_list_htabg_gate_biasP_kernel(
                 for t in range(t0, t0 + per_bank):
                     nc.scalar.activation(y32[:, t, :], y[:, t - t0, :], ACT.Identity, bias=bias[:, t : t + 1])
             nc.sync.dma_start(out_rows[:, :, j0 : j0 + w], y32[:])
-            y16 = held([P, PACK * w], BF16, "y16_%d" % c)
-            interleave(nc.scalar.copy if c == 0 else nc.vector.tensor_copy, y16[:], y32[:])
-            yb16[c] = y16
+            yb16[c] = y32
 
         def planes(c):
             j0, w = starts[c], CHUNKS[c]
+            y16 = held([P, PACK * w], BF16, "y16_%d" % c)
+            interleave(nc.scalar.copy if c == 0 else nc.vector.tensor_copy, y16[:], yb16[c][:])
             nc.vector.quantize_mx(
-                out=y_words[:, j0 : j0 + w].bitcast(FP8X4), scales=y_scales[:, j0 : j0 + w], in_=yb16[c][:]
+                out=y_words[:, j0 : j0 + w].bitcast(FP8X4), scales=y_scales[:, j0 : j0 + w], in_=y16[:]
             )
             nc.sync.dma_start(out_words[:, j0 : j0 + w], y_words[:, j0 : j0 + w])
 
@@ -234,13 +242,13 @@ def tile_list_htabg_gate_biasP_kernel(
         wa = deal_words(wa_raw[:], "wa")
         pick(1)
         wd = deal_words(wd_raw[:], "wd")
-        for c in range(2, n):
-            pick(c)
-        stages = [planes, second_layer, first_layer]
-        for step in range(n + len(stages) - 1):
-            for depth, stage in enumerate(stages):
-                c = step - (len(stages) - 1 - depth)
-                if 0 <= c < n:
-                    stage(c)
+        pick(2)
+        for c in range(n):
+            first_layer(c)
+            second_layer(c)
+            if c == 0:
+                pick(3)
+        for c in range(n):
+            planes(c)
         for q in range(QUADS):
-            nc.sync.dma_start(out_2[0, 4 * q : 4 * q + 4, :].bitcast(I32), y_scales[32 * q : 32 * q + 4, :].bitcast(I32))
+            (nc.sync if q % 2 else nc.scalar).dma_start(out_2[0, 4 * q : 4 * q + 4, :].bitcast(I32), y_scales[32 * q : 32 * q + 4, :].bitcast(I32))

@@ -23,7 +23,6 @@ BANK = 512
 SUB = BANK // PACK
 CHUNKS = [256, 256, 256, 256]
 HALF = J // 2
-EARLY = 768
 
 
 def tile_list_htabg_gate_biasP_kernel(
@@ -43,21 +42,21 @@ def tile_list_htabg_gate_biasP_kernel(
             return dram[a].rearrange("p n i -> p (n i)").bitcast(I32)
 
         def staged(shape, dtype, name, kib):
-            return stage_pool.tile(shape, dtype, name=name, align_bytes=64, offset=kib * 1024)
+            return stage_pool.tile(shape, dtype, name=name, align_bytes=64, offset=int(kib * 1024))
 
         def deal_words(raw, name):
             dealt = held([P, R], U32, name)
             nc.scalar.copy(
-                dealt[:].rearrange("p (t m i) -> p m t i", t=PACK, i=4),
-                raw.bitcast(U32).rearrange("p (m i t) -> p m t i", t=PACK, i=4),
+                dealt[:].rearrange("p (t m) -> p m t", t=PACK),
+                raw.bitcast(U32).rearrange("p (m t) -> p m t", t=PACK),
             )
             return dealt
 
         idx = keep.tile([P, J // 16], U16, name="idx")
         idx2 = keep.tile([P, J // 16], U16, name="idx2")
-        w_s_raw = staged([P, R], U8, "w_s_raw", 0)
-        tab_s = staged([P, T], U8, "tab_s", 8)
-        wb_raw = staged([P, 2, R], I32, "wb_raw", 16)
+        w_s_raw = staged([P, R], U8, "w_s_raw", 3.75)
+        tab_s = staged([P, T], U8, "tab_s", 19)
+        wb_raw = held([P, 2, R], I32, "wb_raw")
         tab_w = staged([P, T], I32, "tab_w", 24)
         w_s = held([P, 4 * R], U8, "w_s")
         v_s = held([P, 2 * J], U8, "v_s")
@@ -73,11 +72,7 @@ def tile_list_htabg_gate_biasP_kernel(
         nc.sync.dma_start(tab_s[:32, :].bitcast(I32), tab_scales.bitcast(I32).rearrange("a q n -> q a n"))
         nc.sync.dma_start(tab_w[:], words_of(tab_words, 0))
         nc.sync.dma_start(wb_raw[:], wb_words.rearrange("a p n i -> p a (n i)").bitcast(I32))
-        wgt_lo = held([P, EARLY], F32, "wgt_lo")
-        nc.sync.dma_start(wgt_lo[:], wgt2[:, :EARLY])
         nc.sync.dma_start(idx2[:], offs2)
-        bias = held([P, PACK], F32, "bias")
-        nc.gpsimd.dma_start(bias[:], b.rearrange("(p t) -> p t", t=PACK))
 
         w_s_dealt = held([P, R], U8, "w_s_dealt")
         nc.vector.tensor_copy(
@@ -86,11 +81,14 @@ def tile_list_htabg_gate_biasP_kernel(
         for q in range(QUADS):
             nc.sync.dma_start(w_s[32 * q : 32 * q + 4, :].bitcast(I32), w_s_dealt[16 * q : 16 * q + 16, :].bitcast(I32))
 
+        wgt = staged([P, J], F32, "wgt", 0)
+        nc.sync.dma_start(wgt[:], wgt2)
+
         x_rows = xT.rearrange("(p i) t -> p i t", i=PACK)
         x_planes = []
 
         def load_x(i):
-            plane = staged([P, T], F32, "x%d" % i, 8 * i)
+            plane = staged([P, T], F32, "x%d" % i, (4, 12, 24, 33)[i])
             nc.sync.dma_start(plane[:], x_rows[:, i, :])
             x_planes.append(plane)
 
@@ -100,11 +98,13 @@ def tile_list_htabg_gate_biasP_kernel(
         for q in range(QUADS):
             nc.sync.dma_start(v_s[32 * q : 32 * q + 4, :].bitcast(I32), v_s_picked[8 * q : 8 * q + 8, :].bitcast(I32))
         load_x(1)
+        wad_raw = staged([P, R + N], I32, "wad_raw", 20)
+        nc.sync.dma_start(wad_raw[:, :R], words_of(wa_words, 0))
+        nc.sync.dma_start(wad_raw[:, R:], words_of(wd_words, 0))
         wb = [deal_words(wb_raw[:, a, :], "wb%d" % a) for a in range(2)]
-        load_x(2)
-        both = staged([P, J], U32, "v_both", 33)
+        both = staged([P, J], U32, "v_both", 32)
         nc.vector.tensor_copy(both[:], tab_w[:].bitcast(U32).indirect(idx[:]))
-        load_x(3)
+        load_x(2)
         v_w = []
         for u in range(2):
             parted = held([P, 2, HALF], U16, "v_w%d" % u)
@@ -112,32 +112,30 @@ def tile_list_htabg_gate_biasP_kernel(
                 parted[:], both[:, u * HALF : (u + 1) * HALF].bitcast(U16).rearrange("p (j d) -> p d j", d=2)
             )
             v_w.append(parted)
-        wa_raw = staged([P, R], I32, "wa_raw", 32)
-        wgt_hi = staged([P, J - EARLY], F32, "wgt_hi", 34)
-        wd_raw = staged([P, N], I32, "wd_raw", 36)
-        nc.sync.dma_start(wa_raw[:], words_of(wa_words, 0))
-        nc.sync.dma_start(wgt_hi[:], wgt2[:, EARLY:])
-        nc.sync.dma_start(wd_raw[:], words_of(wd_words, 0))
-        wgt = [wgt_lo, wgt_hi]
+        load_x(3)
+        bias = staged([P, PACK], F32, "bias", 32)
+        nc.sync.dma_start(bias[:], b.rearrange("(p t) -> p t", t=PACK))
 
         gates = []
-        for s in range(J // SUB):
-            u, j0 = divmod(s * SUB, HALF)
-            yb = psum.tile([P, PACK, SUB], F32, name="yb", tag="first")
+        for u in range(2):
+            gate = held([P, PACK, HALF], F32, "gate%d" % u)
             for t in range(PACK):
+                yb = psum.tile([P, HALF], F32, name="yb", tag="first")
                 for a in range(2):
                     nc.tensor.matmul_mx(
-                        out=yb[:, t, :],
+                        out=yb[:],
                         lhsT=wb[a][:, t * P : (t + 1) * P].bitcast(FP8X4),
                         lhsT_scale=w_s[:, a * R + t * P : a * R + (t + 1) * P],
-                        rhs=v_w[u][:, a, j0 : j0 + SUB].bitcast(FP4X4),
-                        rhs_scale=v_s[:, a * J + s * SUB : a * J + (s + 1) * SUB],
+                        rhs=v_w[u][:, a, :].bitcast(FP4X4),
+                        rhs_scale=v_s[:, a * J + u * HALF : a * J + (u + 1) * HALF],
                         start=(a == 0),
                         stop=(a == 1),
                     )
-            gate = held([P, SUB, PACK], F32, "gate%d" % s)
-            nc.scalar.activation(gate[:], yb[:].rearrange("p t j -> p j t"), ACT.Sigmoid)
+                nc.scalar.activation(gate[:, t, :], yb[:], ACT.Sigmoid)
             gates.append(gate)
+
+        wa = deal_words(wad_raw[:, :R], "wa")
+        wd = deal_words(wad_raw[:, R:], "wd")
 
         y_words = held([P, J], I32, "y_words")
         y_scales = held([P, J], U8, "y_scales")
@@ -146,33 +144,25 @@ def tile_list_htabg_gate_biasP_kernel(
 
         def interleave(copy, dst, src):
             copy(
-                dst.rearrange("p (c i t) -> p c t i", t=PACK, i=4),
-                src.rearrange("p t (c i) -> p c t i", i=4),
+                dst.rearrange("p (c i t) -> p c t i", t=PACK, i=2),
+                src.rearrange("p t (c i) -> p c t i", i=2),
             )
 
         starts = [sum(CHUNKS[:c]) for c in range(len(CHUNKS))]
         xq = {}
         hq = {}
+        sums = {}
         yb16 = {}
 
         def pick(c):
             j0, w = starts[c], CHUNKS[c]
-            u, h0 = divmod(j0, EARLY)
             x16 = held([P, PACK * w], BF16, "x16_%d" % c)
-            group = 2 if u == 0 else PACK
-            for i0 in range(0, PACK, group):
-                picked = held([P, group, w], F32, "picked%d_%d" % (c, i0))
-                for i in range(i0, i0 + group):
-                    nc.vector.tensor_tensor(
-                        picked[:, i - i0, :],
-                        x_planes[i][:].indirect(idx2[:, j0 // 16 : (j0 + w) // 16]),
-                        wgt[u][:, h0 : h0 + w],
-                        MULT,
-                    )
-                nc.scalar.copy(
-                    x16[:].rearrange("p (c i t) -> p c t i", t=PACK, i=4)[:, :, i0 : i0 + group, :],
-                    picked[:].rearrange("p t (c i) -> p c t i", i=4),
+            picked = held([P, PACK, w], F32, "picked%d" % c)
+            for i in range(PACK):
+                nc.vector.tensor_tensor(
+                    picked[:, i, :], x_planes[i][:].indirect(idx2[:, j0 // 16 : (j0 + w) // 16]), wgt[:, j0 : j0 + w], MULT
                 )
+            interleave(nc.scalar.copy, x16[:], picked[:])
             xq[c] = x16
 
         def quantise(src, name, w):
@@ -184,7 +174,7 @@ def tile_list_htabg_gate_biasP_kernel(
         def first_layer(c):
             j0, w = starts[c], CHUNKS[c]
             codes, scales = quantise(xq[c], "x%d" % c, w)
-            h16 = held([P, PACK * w], BF16, "h16_%d" % c)
+            sums[c] = []
             for s in range(w // SUB):
                 cols = slice(s * SUB, (s + 1) * SUB)
                 ya = psum.tile([P, PACK, SUB], F32, name="ya", tag="first")
@@ -198,10 +188,17 @@ def tile_list_htabg_gate_biasP_kernel(
                         start=True,
                         stop=True,
                     )
+                sums[c].append(ya)
+
+        def gate_sums(c):
+            j0, w = starts[c], CHUNKS[c]
+            h16 = held([P, PACK * w], BF16, "h16_%d" % c)
+            for s, ya in enumerate(sums[c]):
+                u, g0 = divmod(j0 + s * SUB, HALF)
                 nc.vector.tensor_tensor(
-                    h16[:, s * BANK : (s + 1) * BANK].rearrange("p (j t) -> p j t", t=PACK),
-                    ya[:].rearrange("p t j -> p j t"),
-                    gates[j0 // SUB + s][:],
+                    h16[:, s * BANK : (s + 1) * BANK].rearrange("p (c i t) -> p c t i", t=PACK, i=2),
+                    ya[:].rearrange("p t (c i) -> p c t i", i=2),
+                    gates[u][:, :, g0 : g0 + SUB].rearrange("p t (c i) -> p c t i", i=2),
                     MULT,
                 )
             hq[c] = h16
@@ -239,15 +236,13 @@ def tile_list_htabg_gate_biasP_kernel(
 
         n = len(CHUNKS)
         pick(0)
-        wa = deal_words(wa_raw[:], "wa")
         pick(1)
-        wd = deal_words(wd_raw[:], "wd")
-        pick(2)
         for c in range(n):
             first_layer(c)
+            if c + 2 < n:
+                pick(c + 2)
+            gate_sums(c)
             second_layer(c)
-            if c == 0:
-                pick(3)
         for c in range(n):
             planes(c)
         for q in range(QUADS):

@@ -88,7 +88,7 @@ def tile_list_htabg_gate_biasP_kernel(
         x_planes = []
 
         def load_x(i):
-            plane = staged([P, T], F32, "x%d" % i, (4, 12, 24, 33)[i])
+            plane = staged([P, T], F32, "x%d" % i, (4, 12, 24, 35)[i])
             nc.sync.dma_start(plane[:], x_rows[:, i, :])
             x_planes.append(plane)
 
@@ -98,11 +98,10 @@ def tile_list_htabg_gate_biasP_kernel(
         for q in range(QUADS):
             nc.sync.dma_start(v_s[32 * q : 32 * q + 4, :].bitcast(I32), v_s_picked[8 * q : 8 * q + 8, :].bitcast(I32))
         load_x(1)
-        wad_raw = staged([P, R + N], I32, "wad_raw", 20)
-        nc.sync.dma_start(wad_raw[:, :R], words_of(wa_words, 0))
-        nc.sync.dma_start(wad_raw[:, R:], words_of(wd_words, 0))
+        wa_raw = staged([P, R], I32, "wa_raw", 20)
+        nc.sync.dma_start(wa_raw[:], words_of(wa_words, 0))
         wb = [deal_words(wb_raw[:, a, :], "wb%d" % a) for a in range(2)]
-        both = staged([P, J], U32, "v_both", 32)
+        both = staged([P, J], U32, "v_both", 34)
         nc.vector.tensor_copy(both[:], tab_w[:].bitcast(U32).indirect(idx[:]))
         load_x(2)
         v_w = []
@@ -113,7 +112,9 @@ def tile_list_htabg_gate_biasP_kernel(
             )
             v_w.append(parted)
         load_x(3)
-        bias = staged([P, PACK], F32, "bias", 32)
+        wd_raw = staged([P, N], I32, "wd_raw", 32.5)
+        nc.sync.dma_start(wd_raw[:], words_of(wd_words, 0))
+        bias = staged([P, PACK], F32, "bias", 34.5)
         nc.sync.dma_start(bias[:], b.rearrange("(p t) -> p t", t=PACK))
 
         gates = []
@@ -134,8 +135,7 @@ def tile_list_htabg_gate_biasP_kernel(
                 nc.scalar.activation(gate[:, t, :], yb[:], ACT.Sigmoid)
             gates.append(gate)
 
-        wa = deal_words(wad_raw[:, :R], "wa")
-        wd = deal_words(wad_raw[:, R:], "wd")
+        wa = deal_words(wa_raw[:], "wa")
 
         y_words = held([P, J], I32, "y_words")
         y_scales = held([P, J], U8, "y_scales")
@@ -154,15 +154,21 @@ def tile_list_htabg_gate_biasP_kernel(
         sums = {}
         yb16 = {}
 
+        picked = held([P, PACK, J], F32, "picked")
+
+        def gather(i, j0, w):
+            nc.vector.tensor_tensor(
+                picked[:, i, j0 : j0 + w], x_planes[i][:].indirect(idx2[:, j0 // 16 : (j0 + w) // 16]), wgt[:, j0 : j0 + w], MULT
+            )
+
+        for i in range(PACK - 1):
+            gather(i, 0, J)
+
         def pick(c):
             j0, w = starts[c], CHUNKS[c]
             x16 = held([P, PACK * w], BF16, "x16_%d" % c)
-            picked = held([P, PACK, w], F32, "picked%d" % c)
-            for i in range(PACK):
-                nc.vector.tensor_tensor(
-                    picked[:, i, :], x_planes[i][:].indirect(idx2[:, j0 // 16 : (j0 + w) // 16]), wgt[:, j0 : j0 + w], MULT
-                )
-            interleave(nc.scalar.copy, x16[:], picked[:])
+            gather(PACK - 1, j0, w)
+            interleave(nc.scalar.copy, x16[:], picked[:, :, j0 : j0 + w])
             xq[c] = x16
 
         def quantise(src, name, w):
@@ -237,6 +243,7 @@ def tile_list_htabg_gate_biasP_kernel(
         n = len(CHUNKS)
         pick(0)
         pick(1)
+        wd = deal_words(wd_raw[:], "wd")
         for c in range(n):
             first_layer(c)
             if c + 2 < n:

from contextlib import ExitStack

import concourse.mybir as mybir

K, L, R, N, T, J = 512, 1024, 512, 512, 2048, 1024
FLOPS = 2 * J * (K * R + L * R + R * N)

F32 = mybir.dt.float32
BF16 = mybir.dt.bfloat16
I32 = mybir.dt.int32
U32 = mybir.dt.uint32
U16 = mybir.dt.uint16
U8 = mybir.dt.uint8
FP8X4 = mybir.dt.float8_e4m3fn_x4
FP4X4 = mybir.dt.float4_e2m1fn_x4
ACT = mybir.ActivationFunctionType
MULT = mybir.AluOpType.mult

P = 128
PACK = 4
QUADS = 4
BANK = 512
SUB = BANK // PACK
CHUNKS = [256, 256, 256, 256]
HALF = J // 2


def tile_list_htabg_gate_biasP_kernel(
    tc, tab_words, tab_scales, xT, wgt2, wa_words, wa_scales, wb_words, wb_scales, wd_words, wd_scales, b, offs, offs2,
    out_0, out_1, out_2,
):
    nc = tc.nc
    with ExitStack() as ctx:
        keep = ctx.enter_context(tc.tile_pool(name="keep", bufs=1))
        stage_pool = ctx.enter_context(tc.tile_pool(name="stage", bufs=1))
        psum = ctx.enter_context(tc.psum_pool(name="psum", bufs=4))

        def held(shape, dtype, name):
            return keep.tile(shape, dtype, name=name, align_bytes=64)

        def words_of(dram, a):
            return dram[a].rearrange("p n i -> p (n i)").bitcast(I32)

        def staged(shape, dtype, name, kib):
            return stage_pool.tile(shape, dtype, name=name, align_bytes=64, offset=int(kib * 1024))

        def deal_words(raw, name):
            dealt = held([P, R], U32, name)
            nc.scalar.copy(
                dealt[:].rearrange("p (t m) -> p m t", t=PACK),
                raw.bitcast(U32).rearrange("p (m t) -> p m t", t=PACK),
            )
            return dealt

        idx = keep.tile([P, J // 16], U16, name="idx")
        idx2 = keep.tile([P, J // 16], U16, name="idx2")
        w_s_raw = staged([P, R], U8, "w_s_raw", 3.75)
        tab_s = staged([P, T], U8, "tab_s", 19)
        wb_raw = held([P, 2, R], I32, "wb_raw")
        tab_w = staged([P, T], I32, "tab_w", 24)
        w_s = held([P, 4 * R], U8, "w_s")
        v_s = held([P, 2 * J], U8, "v_s")
        nc.vector.memset(w_s_raw[64:, :].bitcast(I32), 0)
        nc.vector.memset(tab_s[32:64, :].bitcast(I32), 0)
        nc.vector.memset(tab_s[64:, :].bitcast(I32), 0)
        nc.vector.memset(w_s[:].bitcast(I32), 0)
        nc.vector.memset(v_s[:].bitcast(I32), 0)

        for k, rows in enumerate((wb_scales[0], wb_scales[1], wa_scales[0], wd_scales[0])):
            nc.sync.dma_start(w_s_raw[k:64:4, :].bitcast(I32), rows.bitcast(I32))
        nc.sync.dma_start(idx[:], offs)
        nc.sync.dma_start(tab_s[:32, :].bitcast(I32), tab_scales.bitcast(I32).rearrange("a q n -> q a n"))
        nc.sync.dma_start(tab_w[:], words_of(tab_words, 0))
        nc.sync.dma_start(wb_raw[:], wb_words.rearrange("a p n i -> p a (n i)").bitcast(I32))
        nc.sync.dma_start(idx2[:], offs2)

        w_s_dealt = held([P, R], U8, "w_s_dealt")
        nc.vector.tensor_copy(
            w_s_dealt[:].rearrange("p (t m) -> p t m", t=PACK), w_s_raw[:].rearrange("p (m t) -> p t m", t=PACK)
        )
        for q in range(QUADS):
            nc.sync.dma_start(w_s[32 * q : 32 * q + 4, :].bitcast(I32), w_s_dealt[16 * q : 16 * q + 16, :].bitcast(I32))

        wgt = staged([P, J], F32, "wgt", 0)
        nc.sync.dma_start(wgt[:], wgt2)

        x_rows = xT.rearrange("(p i) t -> p i t", i=PACK)
        x_planes = []

        def load_x(i):
            plane = staged([P, T], F32, "x%d" % i, (4, 12, 24, 35)[i])
            nc.sync.dma_start(plane[:], x_rows[:, i, :])
            x_planes.append(plane)

        load_x(0)
        v_s_picked = held([P, J], U8, "v_s_picked")
        nc.vector.tensor_copy(v_s_picked[:], tab_s[:].indirect(idx[:]))
        for q in range(QUADS):
            nc.sync.dma_start(v_s[32 * q : 32 * q + 4, :].bitcast(I32), v_s_picked[8 * q : 8 * q + 8, :].bitcast(I32))
        load_x(1)
        wa_raw = staged([P, R], I32, "wa_raw", 20)
        nc.sync.dma_start(wa_raw[:], words_of(wa_words, 0))
        wb = [deal_words(wb_raw[:, a, :], "wb%d" % a) for a in range(2)]
        both = staged([P, J], U32, "v_both", 34)
        nc.vector.tensor_copy(both[:], tab_w[:].bitcast(U32).indirect(idx[:]))
        load_x(2)
        v_w = []
        for u in range(2):
            parted = held([P, 2, HALF], U16, "v_w%d" % u)
            nc.vector.tensor_copy(
                parted[:], both[:, u * HALF : (u + 1) * HALF].bitcast(U16).rearrange("p (j d) -> p d j", d=2)
            )
            v_w.append(parted)
        load_x(3)
        wd_raw = staged([P, N], I32, "wd_raw", 32.5)
        nc.sync.dma_start(wd_raw[:], words_of(wd_words, 0))
        bias = staged([P, PACK], F32, "bias", 34.5)
        nc.sync.dma_start(bias[:], b.rearrange("(p t) -> p t", t=PACK))

        gates = []
        for u in range(2):
            gate = held([P, PACK, HALF], F32, "gate%d" % u)
            for t in range(PACK):
                yb = psum.tile([P, HALF], F32, name="yb", tag="first")
                for a in range(2):
                    nc.tensor.matmul_mx(
                        out=yb[:],
                        lhsT=wb[a][:, t * P : (t + 1) * P].bitcast(FP8X4),
                        lhsT_scale=w_s[:, a * R + t * P : a * R + (t + 1) * P],
                        rhs=v_w[u][:, a, :].bitcast(FP4X4),
                        rhs_scale=v_s[:, a * J + u * HALF : a * J + (u + 1) * HALF],
                        start=(a == 0),
                        stop=(a == 1),
                    )
                nc.scalar.activation(gate[:, t, :], yb[:], ACT.Sigmoid)
            gates.append(gate)

        wa = deal_words(wa_raw[:], "wa")

        y_words = held([P, J], I32, "y_words")
        y_scales = held([P, J], U8, "y_scales")
        out_rows = out_0.rearrange("(p t) j -> p t j", t=PACK)
        out_words = words_of(out_1, 0)

        def interleave(copy, dst, src):
            copy(
                dst.rearrange("p (c i t) -> p c t i", t=PACK, i=2),
                src.rearrange("p t (c i) -> p c t i", i=2),
            )

        starts = [sum(CHUNKS[:c]) for c in range(len(CHUNKS))]
        xq = {}
        hq = {}
        sums = {}
        yb16 = {}

        picked = held([P, PACK, J], F32, "picked")

        def gather(i, j0, w):
            nc.vector.tensor_tensor(
                picked[:, i, j0 : j0 + w], x_planes[i][:].indirect(idx2[:, j0 // 16 : (j0 + w) // 16]), wgt[:, j0 : j0 + w], MULT
            )

        for i in range(PACK - 1):
            gather(i, 0, J)

        def pick(c):
            j0, w = starts[c], CHUNKS[c]
            x16 = held([P, PACK * w], BF16, "x16_%d" % c)
            gather(PACK - 1, j0, w)
            interleave(nc.scalar.copy, x16[:], picked[:, :, j0 : j0 + w])
            xq[c] = x16

        def quantise(src, name, w):
            codes = held([P, w], U32, name + "_codes")
            scales = held([P, w], U8, name + "_scales")
            nc.vector.quantize_mx(out=codes[:].bitcast(FP8X4), scales=scales[:], in_=src[:])
            return codes, scales

        def first_layer(c):
            j0, w = starts[c], CHUNKS[c]
            codes, scales = quantise(xq[c], "x%d" % c, w)
            sums[c] = []
            for s in range(w // SUB):
                cols = slice(s * SUB, (s + 1) * SUB)
                ya = psum.tile([P, PACK, SUB], F32, name="ya", tag="first")
                for t in range(PACK):
                    nc.tensor.matmul_mx(
                        out=ya[:, t, :],
                        lhsT=wa[:, t * P : (t + 1) * P].bitcast(FP8X4),
                        lhsT_scale=w_s[:, 2 * R + t * P : 2 * R + (t + 1) * P],
                        rhs=codes[:, cols].bitcast(FP8X4),
                        rhs_scale=scales[:, cols],
                        start=True,
                        stop=True,
                    )
                sums[c].append(ya)

        def gate_sums(c):
            j0, w = starts[c], CHUNKS[c]
            h16 = held([P, PACK * w], BF16, "h16_%d" % c)
            for s, ya in enumerate(sums[c]):
                u, g0 = divmod(j0 + s * SUB, HALF)
                nc.vector.tensor_tensor(
                    h16[:, s * BANK : (s + 1) * BANK].rearrange("p (c i t) -> p c t i", t=PACK, i=2),
                    ya[:].rearrange("p t (c i) -> p c t i", i=2),
                    gates[u][:, :, g0 : g0 + SUB].rearrange("p t (c i) -> p c t i", i=2),
                    MULT,
                )
            hq[c] = h16

        def second_layer(c):
            j0, w = starts[c], CHUNKS[c]
            codes, scales = quantise(hq[c], "h%d" % c, w)
            y32 = held([P, PACK, w], F32, "y32_%d" % c)
            per_bank = BANK // w
            for t0 in range(0, PACK, per_bank):
                y = psum.tile([P, per_bank, w], F32, name="y", tag="second")
                for t in range(t0, t0 + per_bank):
                    nc.tensor.matmul_mx(
                        out=y[:, t - t0, :],
                        lhsT=wd[:, t * P : (t + 1) * P].bitcast(FP8X4),
                        lhsT_scale=w_s[:, 3 * R + t * P : 3 * R + (t + 1) * P],
                        rhs=codes[:].bitcast(FP8X4),
                        rhs_scale=scales[:],
                        start=True,
                        stop=True,
                    )
                for t in range(t0, t0 + per_bank):
                    nc.scalar.activation(y32[:, t, :], y[:, t - t0, :], ACT.Identity, bias=bias[:, t : t + 1])
            nc.sync.dma_start(out_rows[:, :, j0 : j0 + w], y32[:])
            yb16[c] = y32

        def planes(c):
            j0, w = starts[c], CHUNKS[c]
            y16 = held([P, PACK * w], BF16, "y16_%d" % c)
            interleave(nc.scalar.copy if c == 0 else nc.vector.tensor_copy, y16[:], yb16[c][:])
            nc.vector.quantize_mx(
                out=y_words[:, j0 : j0 + w].bitcast(FP8X4), scales=y_scales[:, j0 : j0 + w], in_=y16[:]
            )
            nc.sync.dma_start(out_words[:, j0 : j0 + w], y_words[:, j0 : j0 + w])

        n = len(CHUNKS)
        pick(0)
        pick(1)
        wd = deal_words(wd_raw[:], "wd")
        for c in range(n):
            first_layer(c)
            if c + 2 < n:
                pick(c + 2)
            gate_sums(c)
            second_layer(c)
        for c in range(n):
            planes(c)
        for q in range(QUADS):
            (nc.sync if q % 2 else nc.scalar).dma_start(out_2[0, 4 * q : 4 * q + 4, :].bitcast(I32), y_scales[32 * q : 32 * q + 4, :].bitcast(I32))
